import numpy as np
import ml_dtypes


def mxq(x, axis, fmt="e4m3"):
    dtype, down = {"e4m3": (ml_dtypes.float8_e4m3fn, 7), "e5m2": (ml_dtypes.float8_e5m2, 14)}[fmt]
    v = np.moveaxis(np.asarray(x, np.float32).astype(ml_dtypes.bfloat16).astype(np.float64), axis, -1)
    blocks = v.reshape(v.shape[:-1] + (-1, 32))
    amax = np.abs(blocks).max(-1, keepdims=True)
    byte = np.maximum(np.where(amax > 0, np.frexp(amax)[1] - 1 + 127, 0) - down, 1)
    scale = np.exp2(byte - 127.0)
    codes = (blocks / scale).astype(np.float32).astype(dtype).astype(np.float64)
    return np.moveaxis((codes * scale).reshape(v.shape), -1, axis)


WIDE = False


def mx_kscale(k):
    if not WIDE:
        return np.ones(k)
    levels = np.array([10, -10, 5, -5, 0])
    if k % 512:
        return np.exp2(np.random.permutation(np.resize(levels, k // 32))).repeat(32)
    a = np.empty((k // 512, 16))
    for p in range(k // 512):
        a[p, :8] = np.random.permutation(np.resize(levels, 8))
        for g in range(8):
            far = levels[np.abs(levels - a[p, g]) >= 10]
            a[p, g + 8] = far[np.random.randint(len(far))]
    return np.exp2(a.ravel()).repeat(32)


def f64(x):
    return np.asarray(x).astype(np.float64)


def striped(idx):
    return np.tile(idx.reshape(-1, 16).T, (8, 1)).astype(np.uint16)


def unstriped(offs):
    return offs[:16].T.reshape(-1).astype(np.int64)


E2M1 = np.array([0.0, 0.5, 1.0, 1.5, 2.0, 3.0, 4.0, 6.0, -0.0, -0.5, -1.0, -1.5, -2.0, -3.0, -4.0, -6.0])


def pack_weight(w, fmt):
    k, n = w.shape
    w = f64(np.asarray(w, np.float32).astype(ml_dtypes.bfloat16)).reshape(k // 32, 32, n)
    amax = np.abs(w).max(1)
    if fmt == "e4m3":
        byte = np.frexp(amax)[1] - 1 + 127 - 7
    else:
        mant, ex = np.frexp(amax / 6.0)
        byte = np.where(mant > 0.5, ex, ex - 1) + 127
    byte = np.clip(np.where(amax > 0, byte, 1), 1, 254)
    scaled = (w * np.exp2(127.0 - byte)[:, None, :]).reshape(k, n).astype(np.float32)
    by_word = np.ascontiguousarray(scaled.reshape(k // 512, 128, 4, n).transpose(0, 1, 3, 2))
    if fmt == "e4m3":
        words = by_word.astype(ml_dtypes.float8_e4m3fn).view(np.uint8)
    else:
        c = by_word.astype(ml_dtypes.float4_e2m1fn).view(np.uint8) & 0xF
        words = (c[..., 0::2] | (c[..., 1::2] << 4)).reshape(k // 512, 128, 2 * n)
    return np.ascontiguousarray(words), np.ascontiguousarray(byte.astype(np.uint8).reshape(k // 512, 16, n))


def unpack_weight(words, scales, fmt):
    g, _, n = scales.shape
    words = np.ascontiguousarray(words).reshape(g, 128, n, -1)
    if fmt == "e4m3":
        vals = words.view(ml_dtypes.float8_e4m3fn).astype(np.float64)
    else:
        nib = np.empty((g, 128, n, 4), np.uint8)
        nib[..., 0::2] = words & 0xF
        nib[..., 1::2] = words >> 4
        vals = E2M1[nib]
    vals = vals * np.repeat(np.exp2(scales.astype(np.float64) - 127.0), 8, axis=1)[..., None]
    return vals.transpose(0, 1, 3, 2).reshape(g * 512, n)


def gelu(v):
    return 0.5 * v * (1.0 + np.tanh(np.sqrt(2.0 / np.pi) * (v + 0.044715 * v**3)))


def striped8(idx):
    return np.concatenate([v.reshape(-1, 16).T for v in idx]).astype(np.uint16)


def unstriped8(offs):
    return np.stack([offs[16 * g:16 * g + 16].T.reshape(-1) for g in range(8)]).astype(np.int64)


def put_heads(h, wgs, idx8, t2):
    r = np.arange(h.shape[0])
    page = np.zeros((h.shape[0], t2))
    page[r[:, None], idx8[r % 512 // 64]] = wgs[r // 4 % 128] * h
    return page


def bf(x):
    return np.asarray(x, np.float32).astype(ml_dtypes.bfloat16)


def planes(Y):
    n, m = Y.shape
    b = f64(bf(Y)).reshape(n // 32, 32, m)
    amax = np.abs(b).max(1)
    byte = np.clip(np.where(amax > 0, np.frexp(amax)[1] - 1 + 127 - 7, 1), 1, 254)
    codes = (b * np.exp2(127.0 - byte)[:, None, :]).reshape(n, m).astype(np.float32).astype(ml_dtypes.float8_e4m3fn).view(np.uint8)
    words = codes.reshape(n // 512, 128, 4, m).transpose(0, 1, 3, 2)
    return np.ascontiguousarray(words), np.ascontiguousarray(byte.astype(np.uint8).reshape(n // 512, 16, m))


K, T, S, T2, P, H, N = 1024, 2048, 1024, 2048, 1024, 512, 1024

def setup_inputs():
    n = np.random.standard_normal
    s = mx_kscale(K)[:, None]
    u = mx_kscale(H)[:, None]
    gn = np.exp(0.8 * n(N))
    tab_words, tab_scales = pack_weight(n((K, T)) * s, "e4m3")
    wq_words, wq_scales = pack_weight(0.52 * n((K, H)) / np.sqrt(K) / s, "e2m1")
    wo_words, wo_scales = pack_weight(n((H, N)) / np.sqrt(H) / u * gn, "e4m3")
    return {
        "tab_words": tab_words, "tab_scales": tab_scales,
        "offs": striped(np.random.permutation(T)[:S]),
        "wp": (0.8 * n((K, H)) / np.sqrt(K) / s * u.T).astype(np.float32),
        "wq_words": wq_words, "wq_scales": wq_scales,
        "wgs": np.repeat(np.random.uniform(0.5, 2.0, (8, S)), 16, axis=0).astype(np.float32),
        "offs2": striped8(np.stack([np.random.permutation(T2)[:S] for _ in range(8)])),
        "offs3": striped(np.random.permutation(T2)[:P]),
        "ceiling": ((1.0 + 1.5 * n((H, P))) * u).astype(np.float32),
        "wo_words": wo_words, "wo_scales": wo_scales,
        "shift": (0.5 * n((N, P)) * gn[:, None]).astype(np.float32),
    }

def reference(tab_words, tab_scales, offs, wp, wq_words, wq_scales, wgs, offs2, offs3, ceiling, wo_words, wo_scales, shift):
    v = unpack_weight(tab_words, tab_scales, "e4m3")[:, unstriped(offs)]
    wq = unpack_weight(wq_words, wq_scales, "e2m1")
    wo = unpack_weight(wo_words, wo_scales, "e4m3")
    amp = mxq(f64(wp), 0, "e4m3").T @ v
    ang = wq.T @ v
    h = amp * np.cos(ang) + np.abs(amp)
    page = put_heads(h, f64(wgs), unstriped8(offs2), T2)
    x = page[:, unstriped(offs3)]
    z = np.minimum(x, f64(ceiling))
    y = (wo.T @ mxq(z, 0, "e4m3")) + f64(shift)
    words, scales = planes(y)
    return y, words, scales

@@ -1,0 +1,230 @@
+from contextlib import ExitStack
+
+import concourse.mybir as mybir
+from concourse.masks import make_identity
+
+K, T, S, T2, M, H, N = 1024, 2048, 1024, 2048, 1024, 512, 1024
+FLOPS = 2 * (2 * K * H * S + H * N * M)
+
+F32 = mybir.dt.float32
+BF16 = mybir.dt.bfloat16
+I32 = mybir.dt.int32
+U32 = mybir.dt.uint32
+U16 = mybir.dt.uint16
+U8 = mybir.dt.uint8
+FP8X4 = mybir.dt.float8_e4m3fn_x4
+FP4X4 = mybir.dt.float4_e2m1fn_x4
+ACT = mybir.ActivationFunctionType
+ALU = mybir.AluOpType
+
+P = 128
+PACK = 4
+PASS = P * PACK
+LANES = 16
+LAST_PASS_GATHERS = (256, 256, 512)
+SCATTER_WIDTHS = (128,) * 8
+CHUNK = 256
+
+
+def interleaved(tile):
+    return tile.rearrange("p (c i) t -> p c t i", i=PACK)
+
+
+def by_rows(tile):
+    return tile.rearrange("p t (c i) -> p c t i", i=PACK)
+
+
+def tile_list_swell_trace_features_kernel(
+    tc, tab_words, tab_scales, offs, wp, wq_words, wq_scales, wgs, offs2, offs3, ceiling, wo_words, wo_scales, shift,
+    out_0, out_1, out_2,
+):
+    nc = tc.nc
+    with ExitStack() as ctx:
+        keep = ctx.enter_context(tc.tile_pool(name="keep", bufs=1))
+        ring = ctx.enter_context(tc.tile_pool(name="ring", bufs=2))
+        psum = ctx.enter_context(tc.psum_pool(name="psum", bufs=1))
+
+        def held(shape, dtype, name):
+            return keep.tile(shape, dtype, name=name, align_bytes=64)
+
+        def load_scale_rows(queue, plane, scales):
+            for q in range(4):
+                queue.dma_start(
+                    plane[32 * q : 32 * q + 4].bitcast(I32),
+                    scales[:, 4 * q : 4 * q + 4, :].rearrange("a r c -> r a c").bitcast(I32),
+                )
+
+        def entries(offsets, start, count):
+            return offsets[:, start // LANES : (start + count) // LANES]
+
+        idx = held([P, S // LANES], U16, "idx")
+        idx2 = held([P, S // LANES], U16, "idx2")
+        idx3 = held([P, M // LANES], U16, "idx3")
+        tab_s = held([P, 2, T], U8, "tab_s")
+        wq_s = held([P, 2, H], U8, "wq_s")
+        wo_s = held([P, 1, N], U8, "wo_s")
+        tab_w = [held([P, T], U32, f"tab_w{a}") for a in range(2)]
+        wq_w = held([P, 2, 2 * H], U8, "wq_w")
+        wo_w = held([P, N], I32, "wo_w")
+        wp_parts = [(0, 0, H), (1, 0, H)]
+        wp_raw = [held([P, PACK, w], F32, f"wp_raw{n}") for n, (a, c0, w) in enumerate(wp_parts)]
+        gain = held([P, S], F32, "gain")
+        cap = [held([P, PACK, CHUNK], F32, f"cap{c}") for c in range(M // CHUNK)]
+        y = [[held([P, PACK, CHUNK], F32, f"y{c}_{g}") for g in range(2)] for c in range(M // CHUNK)]
+        pages = [held([P, T2], F32, f"page{i}") for i in range(PACK)]
+        ident = held([P, P], F32, "ident")
+
+        nc.vector.memset(tab_s[:].bitcast(I32), 0)
+        nc.gpsimd.memset(wq_s[:].bitcast(I32), 0)
+        nc.gpsimd.memset(wo_s[:].bitcast(I32), 0)
+        for i in range(PACK):
+            nc.vector.memset(pages[i][:], 0.0)
+
+        def load_wp(n):
+            a, c0, w = wp_parts[n]
+            rows = wp[PASS * a : PASS * (a + 1), c0 : c0 + w]
+            nc.sync.dma_start(wp_raw[n][:], rows.rearrange("(p j) c -> p j c", j=PACK))
+
+        def load_tab(a):
+            nc.sync.dma_start(tab_w[a][:].bitcast(I32), tab_words[a].rearrange("p t i -> p (t i)").bitcast(I32))
+
+        nc.sync.dma_start(idx[:], offs)
+        nc.sync.dma_start(idx2[:], offs2)
+        nc.sync.dma_start(idx3[:], offs3)
+        nc.sync.dma_start(wq_w[:].bitcast(I32), wq_words.rearrange("a p c -> p a c").bitcast(I32))
+        load_scale_rows(nc.scalar, tab_s, tab_scales)
+        load_scale_rows(nc.gpsimd, wq_s, wq_scales)
+        make_identity(nc, ident[:])
+        load_scale_rows(nc.gpsimd, wo_s, wo_scales)
+        load_wp(0)
+        load_tab(0)
+        load_wp(1)
+        load_tab(1)
+        nc.sync.dma_start(gain[:], wgs)
+        nc.sync.dma_start(wo_w[:], wo_words[0].rearrange("p c i -> p (c i)").bitcast(I32))
+        for c in range(M // CHUNK):
+            cols = slice(CHUNK * c, CHUNK * (c + 1))
+            nc.sync.dma_start(cap[c][:], ceiling[:, cols].rearrange("(p t) m -> p t m", t=PACK))
+            for g in range(2):
+                rows = shift[PASS * g : PASS * (g + 1), cols]
+                nc.sync.dma_start(y[c][g][:], rows.rearrange("(p t) m -> p t m", t=PACK))
+
+        v_s = held([P, 2, S], U8, "v_s")
+        v_w = [held([P, S], U32, f"v_w{a}") for a in range(2)]
+        for a in range(2):
+            nc.vector.tensor_copy(v_s[:, a, :], tab_s[:, a, :].indirect(idx[:]))
+
+        wp_c = held([P, 2, H], U32, "wp_c")
+        wp_s = held([P, 2, H], U8, "wp_s")
+
+        def quantise_wp(n, copy):
+            a, c0, w = wp_parts[n]
+            grouped = held([P, w, PACK], BF16, f"wp_bf{n}")
+            copy(interleaved(grouped[:]), by_rows(wp_raw[n][:]))
+            nc.vector.quantize_mx(
+                out=wp_c[:, a, c0 : c0 + w].bitcast(FP8X4),
+                scales=wp_s[:, a, c0 : c0 + w],
+                in_=grouped[:].rearrange("p c t -> p (c t)"),
+            )
+
+        quantise_wp(0, nc.scalar.copy)
+        nc.vector.tensor_copy(v_w[0][:], tab_w[0][:].indirect(idx[:]))
+        quantise_wp(1, nc.scalar.copy)
+        start = 0
+        for count in LAST_PASS_GATHERS:
+            nc.vector.tensor_copy(v_w[1][:, start : start + count], tab_w[1][:].indirect(entries(idx, start, count)))
+            start = start + count
+
+        def features(j0, h_cols):
+            cols = slice(j0, j0 + P)
+            ang = psum.tile([P, H], F32, name="ang", tag="acc", bufs=6)
+            amp = psum.tile([P, H], F32, name="amp", tag="acc", bufs=6)
+            for a in (1, 0):
+                nc.tensor.matmul_mx(
+                    out=ang[:], lhsT=v_w[a][:, cols].bitcast(FP8X4), lhsT_scale=v_s[:, a, cols],
+                    rhs=wq_w[:, a, :].bitcast(FP4X4), rhs_scale=wq_s[:, a, :], start=(a == 1), stop=(a == 0),
+                )
+            for a in (1, 0):
+                nc.tensor.matmul_mx(
+                    out=amp[:], lhsT=v_w[a][:, cols].bitcast(FP8X4), lhsT_scale=v_s[:, a, cols],
+                    rhs=wp_c[:, a, :].bitcast(FP8X4), rhs_scale=wp_s[:, a, :], start=(a == 1), stop=(a == 0),
+                )
+            sq = ring.tile([P, PACK, P], F32, name="sq", bufs=3)
+            pos = ring.tile([P, PACK, P], F32, name="pos", bufs=3)
+            neg = ring.tile([P, PACK, P], F32, name="neg", bufs=3)
+            amp_dealt = amp[:].rearrange("j (q i) -> j i q", i=PACK)
+            nc.scalar.activation(sq[:], ang[:].rearrange("j (q i) -> j i q", i=PACK), ACT.Sin, scale=0.5)
+            nc.scalar.activation(sq[:], sq[:], ACT.Square)
+            nc.scalar.activation(pos[:], amp_dealt, ACT.Relu, scale=2.0)
+            nc.vector.scalar_tensor_tensor(neg[:], amp_dealt, -2.0, sq[:], ALU.mult, ALU.mult)
+            turned = psum.tile([P, PACK, P], F32, name="turned", bufs=2)
+            for i in range(PACK):
+                nc.tensor.matmul(turned[:, i, :], pos[:, i, :], ident[:], start=True, stop=False, is_transpose=True)
+                nc.tensor.matmul(turned[:, i, :], neg[:, i, :], ident[:], start=False, stop=True, is_transpose=True)
+            nc.scalar.copy(h_cols, turned[:])
+
+        start = 0
+        for count in SCATTER_WIDTHS:
+            h = ring.tile([P, PACK, count], F32, name="h", bufs=3)
+            for b in range(count // P):
+                features(start + P * b, h[:, :, P * b : P * (b + 1)])
+            for i in range(PACK):
+                nc.vector.tensor_tensor(
+                    pages[i][:].indirect(entries(idx2, start, count)), h[:, i, :], gain[:, start : start + count],
+                    ALU.mult,
+                )
+            start = start + count
+
+        wo_dw = held([P, N], I32, "wo_dw")
+        wo_ds = held([P, N], U8, "wo_ds")
+        nc.vector.tensor_copy(
+            wo_dw[:].rearrange("p (g t q) -> p g q t", g=2, t=PACK), wo_w[:].rearrange("p (g q t) -> p g q t", g=2, t=PACK)
+        )
+        nc.vector.tensor_copy(
+            wo_ds[:].rearrange("p (g t q) -> p g q t", g=2, t=PACK),
+            wo_s[:, 0, :].rearrange("p (g q t) -> p g q t", g=2, t=PACK),
+        )
+
+        y_s = held([P, 2, M], U8, "y_s")
+        for c in range(M // CHUNK):
+            cols = slice(CHUNK * c, CHUNK * (c + 1))
+            x = ring.tile([P, PACK, CHUNK], F32, name="x")
+            for i in range(PACK):
+                nc.vector.tensor_copy(x[:, i, :], pages[i][:].indirect(entries(idx3, CHUNK * c, CHUNK)))
+            z = ring.tile([P, PACK, CHUNK], BF16, name="z")
+            nc.vector.tensor_tensor(z[:], x[:], cap[c][:], ALU.min)
+            z_grouped = ring.tile([P, CHUNK, PACK], BF16, name="z_grouped", align_bytes=64)
+            nc.scalar.copy(interleaved(z_grouped[:]), by_rows(z[:]))
+            z_c = ring.tile([P, CHUNK], U32, name="z_c", align_bytes=64)
+            z_s = ring.tile([P, CHUNK], U8, name="z_s", align_bytes=64)
+            nc.vector.quantize_mx(
+                out=z_c[:].bitcast(FP8X4), scales=z_s[:], in_=z_grouped[:].rearrange("p c t -> p (c t)")
+            )
+            for g in range(2):
+                for half in range(2):
+                    acc = psum.tile([P, 2, CHUNK], F32, name="acc", tag="acc", bufs=6)
+                    for u in range(2):
+                        n0 = PASS * g + P * (2 * half + u)
+                        nc.tensor.matmul_mx(
+                            out=acc[:, u, :], lhsT=wo_dw[:, n0 : n0 + P].bitcast(FP8X4), lhsT_scale=wo_ds[:, n0 : n0 + P],
+                            rhs=z_c[:].bitcast(FP8X4), rhs_scale=z_s[:], start=True, stop=True,
+                        )
+                    rows = y[c][g][:, 2 * half : 2 * half + 2, :]
+                    nc.vector.tensor_tensor(rows, acc[:], rows, ALU.add)
+                nc.sync.dma_start(
+                    out_0[PASS * g : PASS * (g + 1), cols].rearrange("(p t) m -> p t m", t=PACK), y[c][g][:]
+                )
+                y_grouped = ring.tile([P, CHUNK, PACK], BF16, name="y_grouped", align_bytes=64, bufs=3)
+                nc.scalar.copy(interleaved(y_grouped[:]), by_rows(y[c][g][:]))
+                y_c = ring.tile([P, CHUNK], U32, name="y_c", align_bytes=64, bufs=4)
+                nc.vector.quantize_mx(
+                    out=y_c[:].bitcast(FP8X4), scales=y_s[:, g, cols], in_=y_grouped[:].rearrange("p c t -> p (c t)")
+                )
+                nc.sync.dma_start(
+                    out_1[g, :, cols, :].rearrange("p m t -> p (m t)").bitcast(I32), y_c[:].bitcast(I32)
+                )
+        for q in range(4):
+            nc.scalar.dma_start(
+                out_2[:, 4 * q : 4 * q + 4, :].rearrange("g r m -> r g m").bitcast(I32),
+                y_s[32 * q : 32 * q + 4].bitcast(I32),
+            )

@@ -22,16 +22,17 @@ PACK = 4
 PASS = P * PACK
 LANES = 16
 LAST_PASS_GATHERS = (256, 256, 512)
-SCATTER_WIDTHS = (128,) * 8
+SCATTER_WIDTHS = (128, 128, 256, 256, 256)
+TURNED_CHUNKS = 3
 CHUNK = 256
 
 
-def interleaved(tile):
-    return tile.rearrange("p (c i) t -> p c t i", i=PACK)
+def interleaved(tile, run=PACK):
+    return tile.rearrange("p (c i) t -> p c t i", i=run)
 
 
-def by_rows(tile):
-    return tile.rearrange("p t (c i) -> p c t i", i=PACK)
+def by_rows(tile, run=PACK):
+    return tile.rearrange("p t (c i) -> p c t i", i=run)
 
 
 def tile_list_swell_trace_features_kernel(
@@ -60,7 +61,8 @@ def tile_list_swell_trace_features_kernel(
         idx = held([P, S // LANES], U16, "idx")
         idx2 = held([P, S // LANES], U16, "idx2")
         idx3 = held([P, M // LANES], U16, "idx3")
-        tab_s = held([P, 2, T], U8, "tab_s")
+        tab_s = held([P, T], U8, "tab_s")
+        v_s_last = held([P, S], U8, "v_s_last")
         wq_s = held([P, 2, H], U8, "wq_s")
         wo_s = held([P, 1, N], U8, "wo_s")
         tab_w = [held([P, T], U32, f"tab_w{a}") for a in range(2)]
@@ -74,11 +76,13 @@ def tile_list_swell_trace_features_kernel(
         pages = [held([P, T2], F32, f"page{i}") for i in range(PACK)]
         ident = held([P, P], F32, "ident")
 
-        nc.vector.memset(tab_s[:].bitcast(I32), 0)
-        nc.gpsimd.memset(wq_s[:].bitcast(I32), 0)
-        nc.gpsimd.memset(wo_s[:].bitcast(I32), 0)
+        nc.gpsimd.memset(tab_s[:].bitcast(I32), 0)
+        make_identity(nc, ident[:])
+        nc.vector.memset(wq_s[:].bitcast(I32), 0)
+        nc.vector.memset(v_s_last[:].bitcast(I32), 0)
+        nc.vector.memset(wo_s[:].bitcast(I32), 0)
         for i in range(PACK):
-            nc.vector.memset(pages[i][:], 0.0)
+            (nc.vector if i < PACK // 2 else nc.gpsimd).memset(pages[i][:], 0.0)
 
         def load_wp(n):
             a, c0, w = wp_parts[n]
@@ -89,30 +93,34 @@ def tile_list_swell_trace_features_kernel(
             nc.sync.dma_start(tab_w[a][:].bitcast(I32), tab_words[a].rearrange("p t i -> p (t i)").bitcast(I32))
 
         nc.sync.dma_start(idx[:], offs)
-        nc.sync.dma_start(idx2[:], offs2)
-        nc.sync.dma_start(idx3[:], offs3)
-        nc.sync.dma_start(wq_w[:].bitcast(I32), wq_words.rearrange("a p c -> p a c").bitcast(I32))
-        load_scale_rows(nc.scalar, tab_s, tab_scales)
-        load_scale_rows(nc.gpsimd, wq_s, wq_scales)
-        make_identity(nc, ident[:])
-        load_scale_rows(nc.gpsimd, wo_s, wo_scales)
-        load_wp(0)
         load_tab(0)
+        for q in range(4):
+            nc.sync.dma_start(
+                tab_s[32 * q : 32 * q + 8].bitcast(I32), tab_scales[:, 4 * q : 4 * q + 4, :].bitcast(I32)
+            )
+        load_wp(0)
+        load_scale_rows(nc.sync, wq_s, wq_scales)
         load_wp(1)
         load_tab(1)
+        nc.sync.dma_start(wq_w[:].bitcast(I32), wq_words.rearrange("a p c -> p a c").bitcast(I32))
+
+        v_s = held([P, S], U8, "v_s")
+        v_w = [held([P, S], U32, f"v_w{a}") for a in range(2)]
+        nc.vector.tensor_copy(v_s[:], tab_s[:].indirect(idx[:]))
+        for q in range(4):
+            nc.sync.dma_start(v_s_last[32 * q : 32 * q + 4].bitcast(I32), v_s[32 * q + 4 : 32 * q + 8].bitcast(I32))
+
+        nc.sync.dma_start(idx2[:], offs2)
         nc.sync.dma_start(gain[:], wgs)
         nc.sync.dma_start(wo_w[:], wo_words[0].rearrange("p c i -> p (c i)").bitcast(I32))
+        load_scale_rows(nc.sync, wo_s, wo_scales)
+        nc.sync.dma_start(idx3[:], offs3)
         for c in range(M // CHUNK):
             cols = slice(CHUNK * c, CHUNK * (c + 1))
             nc.sync.dma_start(cap[c][:], ceiling[:, cols].rearrange("(p t) m -> p t m", t=PACK))
             for g in range(2):
                 rows = shift[PASS * g : PASS * (g + 1), cols]
                 nc.sync.dma_start(y[c][g][:], rows.rearrange("(p t) m -> p t m", t=PACK))
-
-        v_s = held([P, 2, S], U8, "v_s")
-        v_w = [held([P, S], U32, f"v_w{a}") for a in range(2)]
-        for a in range(2):
-            nc.vector.tensor_copy(v_s[:, a, :], tab_s[:, a, :].indirect(idx[:]))
 
         wp_c = held([P, 2, H], U32, "wp_c")
         wp_s = held([P, 2, H], U8, "wp_s")
@@ -127,102 +135,173 @@ def tile_list_swell_trace_features_kernel(
                 in_=grouped[:].rearrange("p c t -> p (c t)"),
             )
 
-        quantise_wp(0, nc.scalar.copy)
         nc.vector.tensor_copy(v_w[0][:], tab_w[0][:].indirect(idx[:]))
+        quantise_wp(0, nc.scalar.copy)
         quantise_wp(1, nc.scalar.copy)
         start = 0
         for count in LAST_PASS_GATHERS:
             nc.vector.tensor_copy(v_w[1][:, start : start + count], tab_w[1][:].indirect(entries(idx, start, count)))
             start = start + count
 
-        def features(j0, h_cols):
-            cols = slice(j0, j0 + P)
+        def add_turned(out, first, second):
+            nc.tensor.matmul(out, first, ident[:], start=True, stop=False, is_transpose=True)
+            nc.tensor.matmul(out, second, ident[:], start=False, stop=True, is_transpose=True)
+
+        def terms(block, parts):
+            cols = slice(P * block, P * (block + 1))
             ang = psum.tile([P, H], F32, name="ang", tag="acc", bufs=6)
             amp = psum.tile([P, H], F32, name="amp", tag="acc", bufs=6)
-            for a in (1, 0):
+            first, last = (0, 1) if block == 0 else (1, 0)
+            for a in (first, last):
                 nc.tensor.matmul_mx(
-                    out=ang[:], lhsT=v_w[a][:, cols].bitcast(FP8X4), lhsT_scale=v_s[:, a, cols],
-                    rhs=wq_w[:, a, :].bitcast(FP4X4), rhs_scale=wq_s[:, a, :], start=(a == 1), stop=(a == 0),
+                    out=ang[:], lhsT=v_w[a][:, cols].bitcast(FP8X4), lhsT_scale=(v_s, v_s_last)[a][:, cols],
+                    rhs=wq_w[:, a, :].bitcast(FP4X4), rhs_scale=wq_s[:, a, :], start=(a == first), stop=(a == last),
                 )
-            for a in (1, 0):
+            for a in (first, last):
                 nc.tensor.matmul_mx(
-                    out=amp[:], lhsT=v_w[a][:, cols].bitcast(FP8X4), lhsT_scale=v_s[:, a, cols],
-                    rhs=wp_c[:, a, :].bitcast(FP8X4), rhs_scale=wp_s[:, a, :], start=(a == 1), stop=(a == 0),
+                    out=amp[:], lhsT=v_w[a][:, cols].bitcast(FP8X4), lhsT_scale=v_s[4 * a : P, cols],
+                    rhs=wp_c[:, a, :].bitcast(FP8X4), rhs_scale=wp_s[:, a, :], start=(a == first), stop=(a == last),
                 )
-            sq = ring.tile([P, PACK, P], F32, name="sq", bufs=3)
-            pos = ring.tile([P, PACK, P], F32, name="pos", bufs=3)
-            neg = ring.tile([P, PACK, P], F32, name="neg", bufs=3)
+            pos = ring.tile([P, PACK, P], F32, name="pos", bufs=4)
+            neg = ring.tile([P, PACK, P], F32, name="neg", bufs=4)
+            ang_dealt = ang[:].rearrange("j (q i) -> j i q", i=PACK)
             amp_dealt = amp[:].rearrange("j (q i) -> j i q", i=PACK)
-            nc.scalar.activation(sq[:], ang[:].rearrange("j (q i) -> j i q", i=PACK), ACT.Sin, scale=0.5)
-            nc.scalar.activation(sq[:], sq[:], ACT.Square)
-            nc.scalar.activation(pos[:], amp_dealt, ACT.Relu, scale=2.0)
-            nc.vector.scalar_tensor_tensor(neg[:], amp_dealt, -2.0, sq[:], ALU.mult, ALU.mult)
-            turned = psum.tile([P, PACK, P], F32, name="turned", bufs=2)
-            for i in range(PACK):
-                nc.tensor.matmul(turned[:, i, :], pos[:, i, :], ident[:], start=True, stop=False, is_transpose=True)
-                nc.tensor.matmul(turned[:, i, :], neg[:, i, :], ident[:], start=False, stop=True, is_transpose=True)
-            nc.scalar.copy(h_cols, turned[:])
+            for n, rows in enumerate(parts):
+                if block == 0:
+                    sq = keep.tile([P, rows.stop - rows.start, P], F32, name="sq", tag=f"dealt{n}", align_bytes=64)
+                else:
+                    sq = ring.tile([P, PACK, P], F32, name="sq")
+                nc.scalar.activation(sq[:], ang_dealt[:, rows, :], ACT.Sin, scale=0.5)
+                nc.scalar.activation(sq[:], sq[:], ACT.Square)
+                nc.scalar.activation(pos[:, rows, :], amp_dealt[:, rows, :], ACT.Relu, scale=2.0)
+                nc.vector.scalar_tensor_tensor(neg[:, rows, :], amp_dealt[:, rows, :], -2.0, sq[:], ALU.mult, ALU.mult)
+            return pos, neg
 
-        start = 0
-        for count in SCATTER_WIDTHS:
+        def turn_back(pos, neg, h_cols, parts):
+            for rows in parts:
+                turned = psum.tile([P, PACK, P], F32, name="turned", bufs=2)
+                for i in range(rows.start, rows.stop):
+                    add_turned(turned[:, i, :], pos[:, i, :], neg[:, i, :])
+                nc.scalar.copy(h_cols[:, rows, :], turned[:, rows, :])
+
+        whole = [slice(0, PACK)]
+        halves = [slice(0, PACK // 2), slice(PACK // 2, PACK)]
+        starts = [sum(SCATTER_WIDTHS[:n]) for n in range(len(SCATTER_WIDTHS) + 1)]
+        made = {}
+
+        def make_terms(upto):
+            for block in range(len(made), min(upto, S) // P):
+                made[block] = terms(block, halves if block == 0 else whole)
+
+        for n, count in enumerate(SCATTER_WIDTHS):
+            start = starts[n]
+            make_terms(start + count + (0 if n == 0 else 2 * P))
             h = ring.tile([P, PACK, count], F32, name="h", bufs=3)
             for b in range(count // P):
-                features(start + P * b, h[:, :, P * b : P * (b + 1)])
+                block = start // P + b
+                turn_back(*made[block], h[:, :, P * b : P * (b + 1)], halves if block == 0 else whole)
             for i in range(PACK):
                 nc.vector.tensor_tensor(
                     pages[i][:].indirect(entries(idx2, start, count)), h[:, i, :], gain[:, start : start + count],
                     ALU.mult,
                 )
-            start = start + count
 
-        wo_dw = held([P, N], I32, "wo_dw")
-        wo_ds = held([P, N], U8, "wo_ds")
+        wo_ds = keep.tile([P, N], U8, name="wo_ds", tag="dealt0", align_bytes=64)
+        wo_dw = keep.tile([P, N], I32, name="wo_dw", tag="dealt1", align_bytes=64)
         nc.vector.tensor_copy(
-            wo_dw[:].rearrange("p (g t q) -> p g q t", g=2, t=PACK), wo_w[:].rearrange("p (g q t) -> p g q t", g=2, t=PACK)
+            wo_dw[:].rearrange("p (g t b q) -> p g b t q", g=2, t=PACK, q=PACK),
+            wo_w[:].rearrange("p (g b q t) -> p g b t q", g=2, t=PACK, q=PACK),
         )
         nc.vector.tensor_copy(
-            wo_ds[:].rearrange("p (g t q) -> p g q t", g=2, t=PACK),
-            wo_s[:, 0, :].rearrange("p (g q t) -> p g q t", g=2, t=PACK),
+            wo_ds[:].rearrange("p (g t q) -> p g t q", g=2, t=PACK),
+            wo_s[:, 0, :].rearrange("p (g q t) -> p g t q", g=2, t=PACK),
         )
+
+        shift_turned = {}
+        for c in range(TURNED_CHUNKS):
+            for b in range(CHUNK // P):
+                turned = psum.tile([P, PACK, P], F32, name="turned", bufs=2)
+                for t in range(PACK):
+                    nc.tensor.transpose(turned[:, t, :], y[c][0][:, t, P * b : P * (b + 1)], ident[:])
+                shift_turned[c, b] = held([P, PACK, P], F32, f"shift_turned{c}_{b}")
+                nc.scalar.copy(shift_turned[c, b][:], turned[:])
 
         y_s = held([P, 2, M], U8, "y_s")
+
+        def add_on_vector(z_c, z_s, g, y_part):
+            width = y_part.shape[2]
+            per_bank = H // width
+            for t0 in range(0, PACK, per_bank):
+                acc = psum.tile([P, per_bank, width], F32, name="acc", tag="acc", bufs=6)
+                for u in range(per_bank):
+                    n0 = PASS * g + P * (t0 + u)
+                    nc.tensor.matmul_mx(
+                        out=acc[:, u, :], lhsT=wo_dw[:, n0 : n0 + P].bitcast(FP8X4), lhsT_scale=wo_ds[:, n0 : n0 + P],
+                        rhs=z_c.bitcast(FP8X4), rhs_scale=z_s, start=True, stop=True,
+                    )
+                rows = y_part[:, t0 : t0 + per_bank, :]
+                nc.vector.tensor_tensor(rows, acc[:], rows, ALU.add)
+
+        def add_on_tensor(z_c, z_s, c):
+            products = []
+            for b in range(CHUNK // P):
+                cols = slice(P * b, P * (b + 1))
+                acc = psum.tile([P, PASS], F32, name="acc", tag="acc", bufs=6)
+                nc.tensor.matmul_mx(
+                    out=acc[:], lhsT=z_c[:, cols].bitcast(FP8X4), lhsT_scale=z_s[:, cols],
+                    rhs=wo_w[:, 0:PASS].bitcast(FP8X4), rhs_scale=wo_s[:, 0, 0:PASS], start=True, stop=True,
+                )
+                product = ring.tile([P, PACK, P], F32, name="product")
+                nc.scalar.copy(product[:], acc[:].rearrange("m (q t) -> m t q", t=PACK))
+                products.append(product)
+            for t0 in range(0, PACK, 2):
+                turned = psum.tile([P, 2, CHUNK], F32, name="turned", bufs=2)
+                for u in range(2):
+                    for b in range(CHUNK // P):
+                        add_turned(
+                            turned[:, u, P * b : P * (b + 1)], products[b][:, t0 + u, :], shift_turned[c, b][:, t0 + u, :]
+                        )
+                nc.scalar.copy(y[c][0][:, t0 : t0 + 2, :], turned[:])
+
+        def hand_out(y_part, g, cols, copy, tag, bufs):
+            width = y_part.shape[2]
+            nc.sync.dma_start(out_0[PASS * g : PASS * (g + 1), cols].rearrange("(p t) m -> p t m", t=PACK), y_part)
+            y_grouped = ring.tile([P, width, PACK], BF16, name="y_grouped", align_bytes=64, tag=tag, bufs=bufs)
+            copy(interleaved(y_grouped[:]), by_rows(y_part))
+            y_c = ring.tile([P, width], U32, name="y_c", align_bytes=64, bufs=4)
+            nc.vector.quantize_mx(
+                out=y_c[:].bitcast(FP8X4), scales=y_s[:, g, cols], in_=y_grouped[:].rearrange("p c t -> p (c t)")
+            )
+            nc.sync.dma_start(out_1[g, :, cols, :].rearrange("p m t -> p (m t)").bitcast(I32), y_c[:].bitcast(I32))
+
+        step = 0
         for c in range(M // CHUNK):
-            cols = slice(CHUNK * c, CHUNK * (c + 1))
-            x = ring.tile([P, PACK, CHUNK], F32, name="x")
+            x = ring.tile([P, PACK, CHUNK], F32, name="x", bufs=1)
             for i in range(PACK):
                 nc.vector.tensor_copy(x[:, i, :], pages[i][:].indirect(entries(idx3, CHUNK * c, CHUNK)))
-            z = ring.tile([P, PACK, CHUNK], BF16, name="z")
-            nc.vector.tensor_tensor(z[:], x[:], cap[c][:], ALU.min)
-            z_grouped = ring.tile([P, CHUNK, PACK], BF16, name="z_grouped", align_bytes=64)
-            nc.scalar.copy(interleaved(z_grouped[:]), by_rows(z[:]))
-            z_c = ring.tile([P, CHUNK], U32, name="z_c", align_bytes=64)
-            z_s = ring.tile([P, CHUNK], U8, name="z_s", align_bytes=64)
-            nc.vector.quantize_mx(
-                out=z_c[:].bitcast(FP8X4), scales=z_s[:], in_=z_grouped[:].rearrange("p c t -> p (c t)")
-            )
-            for g in range(2):
-                for half in range(2):
-                    acc = psum.tile([P, 2, CHUNK], F32, name="acc", tag="acc", bufs=6)
-                    for u in range(2):
-                        n0 = PASS * g + P * (2 * half + u)
-                        nc.tensor.matmul_mx(
-                            out=acc[:, u, :], lhsT=wo_dw[:, n0 : n0 + P].bitcast(FP8X4), lhsT_scale=wo_ds[:, n0 : n0 + P],
-                            rhs=z_c[:].bitcast(FP8X4), rhs_scale=z_s[:], start=True, stop=True,
-                        )
-                    rows = y[c][g][:, 2 * half : 2 * half + 2, :]
-                    nc.vector.tensor_tensor(rows, acc[:], rows, ALU.add)
-                nc.sync.dma_start(
-                    out_0[PASS * g : PASS * (g + 1), cols].rearrange("(p t) m -> p t m", t=PACK), y[c][g][:]
+            width = CHUNK if c < TURNED_CHUNKS else CHUNK // 2
+            for m0 in range(0, CHUNK, width):
+                part = slice(m0, m0 + width)
+                cols = slice(CHUNK * c + m0, CHUNK * c + m0 + width)
+                last = CHUNK * c + m0 + width == M
+                shared = "grouped_last" if last else f"grouped{step % 2}"
+                step = step + 1
+                z_grouped = ring.tile([P, width, PACK], BF16, name="z_grouped", align_bytes=64, tag=shared, bufs=1)
+                nc.vector.tensor_tensor(
+                    interleaved(z_grouped[:], 2), by_rows(x[:, :, part], 2), by_rows(cap[c][:, :, part], 2), ALU.min
                 )
-                y_grouped = ring.tile([P, CHUNK, PACK], BF16, name="y_grouped", align_bytes=64, bufs=3)
-                nc.scalar.copy(interleaved(y_grouped[:]), by_rows(y[c][g][:]))
-                y_c = ring.tile([P, CHUNK], U32, name="y_c", align_bytes=64, bufs=4)
+                z_c = ring.tile([P, width], U32, name="z_c", align_bytes=64)
+                z_s = ring.tile([P, width], U8, name="z_s", align_bytes=64)
                 nc.vector.quantize_mx(
-                    out=y_c[:].bitcast(FP8X4), scales=y_s[:, g, cols], in_=y_grouped[:].rearrange("p c t -> p (c t)")
+                    out=z_c[:].bitcast(FP8X4), scales=z_s[:], in_=z_grouped[:].rearrange("p c t -> p (c t)")
                 )
-                nc.sync.dma_start(
-                    out_1[g, :, cols, :].rearrange("p m t -> p (m t)").bitcast(I32), y_c[:].bitcast(I32)
-                )
+                for g in range(2):
+                    if g == 0 and c < TURNED_CHUNKS:
+                        add_on_tensor(z_c, z_s, c)
+                    else:
+                        add_on_vector(z_c[:], z_s[:], g, y[c][g][:, :, part])
+                    copy = nc.vector.tensor_copy if last and g == 1 else nc.scalar.copy
+                    hand_out(y[c][g][:, :, part], g, cols, copy, *((shared, 1) if g == 0 else ("grouped_second", 2)))
         for q in range(4):
             nc.scalar.dma_start(
                 out_2[:, 4 * q : 4 * q + 4, :].rearrange("g r m -> r g m").bitcast(I32),

from contextlib import ExitStack

import concourse.mybir as mybir
from concourse.masks import make_identity

K, T, S, T2, M, H, N = 1024, 2048, 1024, 2048, 1024, 512, 1024
FLOPS = 2 * (2 * K * H * S + H * N * M)

F32 = mybir.dt.float32
BF16 = mybir.dt.bfloat16
I32 = mybir.dt.int32
U32 = mybir.dt.uint32
U16 = mybir.dt.uint16
U8 = mybir.dt.uint8
FP8X4 = mybir.dt.float8_e4m3fn_x4
FP4X4 = mybir.dt.float4_e2m1fn_x4
ACT = mybir.ActivationFunctionType
ALU = mybir.AluOpType

P = 128
PACK = 4
PASS = P * PACK
LANES = 16
LAST_PASS_GATHERS = (256, 256, 512)
SCATTER_WIDTHS = (128, 128, 256, 256, 256)
TURNED_CHUNKS = 3
CHUNK = 256


def interleaved(tile, run=PACK):
    return tile.rearrange("p (c i) t -> p c t i", i=run)


def by_rows(tile, run=PACK):
    return tile.rearrange("p t (c i) -> p c t i", i=run)


def tile_list_swell_trace_features_kernel(
    tc, tab_words, tab_scales, offs, wp, wq_words, wq_scales, wgs, offs2, offs3, ceiling, wo_words, wo_scales, shift,
    out_0, out_1, out_2,
):
    nc = tc.nc
    with ExitStack() as ctx:
        keep = ctx.enter_context(tc.tile_pool(name="keep", bufs=1))
        ring = ctx.enter_context(tc.tile_pool(name="ring", bufs=2))
        psum = ctx.enter_context(tc.psum_pool(name="psum", bufs=1))

        def held(shape, dtype, name):
            return keep.tile(shape, dtype, name=name, align_bytes=64)

        def load_scale_rows(queue, plane, scales):
            for q in range(4):
                queue.dma_start(
                    plane[32 * q : 32 * q + 4].bitcast(I32),
                    scales[:, 4 * q : 4 * q + 4, :].rearrange("a r c -> r a c").bitcast(I32),
                )

        def entries(offsets, start, count):
            return offsets[:, start // LANES : (start + count) // LANES]

        idx = held([P, S // LANES], U16, "idx")
        idx2 = held([P, S // LANES], U16, "idx2")
        idx3 = held([P, M // LANES], U16, "idx3")
        tab_s = held([P, T], U8, "tab_s")
        v_s_last = held([P, S], U8, "v_s_last")
        wq_s = held([P, 2, H], U8, "wq_s")
        wo_s = held([P, 1, N], U8, "wo_s")
        tab_w = [held([P, T], U32, f"tab_w{a}") for a in range(2)]
        wq_w = held([P, 2, 2 * H], U8, "wq_w")
        wo_w = held([P, N], I32, "wo_w")
        wp_parts = [(0, 0, H), (1, 0, H)]
        wp_raw = [held([P, PACK, w], F32, f"wp_raw{n}") for n, (a, c0, w) in enumerate(wp_parts)]
        gain = held([P, S], F32, "gain")
        cap = [held([P, PACK, CHUNK], F32, f"cap{c}") for c in range(M // CHUNK)]
        y = [[held([P, PACK, CHUNK], F32, f"y{c}_{g}") for g in range(2)] for c in range(M // CHUNK)]
        pages = [held([P, T2], F32, f"page{i}") for i in range(PACK)]
        ident = held([P, P], F32, "ident")

        nc.gpsimd.memset(tab_s[:].bitcast(I32), 0)
        make_identity(nc, ident[:])
        nc.vector.memset(wq_s[:].bitcast(I32), 0)
        nc.vector.memset(v_s_last[:].bitcast(I32), 0)
        nc.vector.memset(wo_s[:].bitcast(I32), 0)
        for i in range(PACK):
            (nc.vector if i < PACK // 2 else nc.gpsimd).memset(pages[i][:], 0.0)

        def load_wp(n):
            a, c0, w = wp_parts[n]
            rows = wp[PASS * a : PASS * (a + 1), c0 : c0 + w]
            nc.sync.dma_start(wp_raw[n][:], rows.rearrange("(p j) c -> p j c", j=PACK))

        def load_tab(a):
            nc.sync.dma_start(tab_w[a][:].bitcast(I32), tab_words[a].rearrange("p t i -> p (t i)").bitcast(I32))

        nc.sync.dma_start(idx[:], offs)
        load_tab(0)
        for q in range(4):
            nc.sync.dma_start(
                tab_s[32 * q : 32 * q + 8].bitcast(I32), tab_scales[:, 4 * q : 4 * q + 4, :].bitcast(I32)
            )
        load_wp(0)
        load_scale_rows(nc.sync, wq_s, wq_scales)
        load_wp(1)
        load_tab(1)
        nc.sync.dma_start(wq_w[:].bitcast(I32), wq_words.rearrange("a p c -> p a c").bitcast(I32))

        v_s = held([P, S], U8, "v_s")
        v_w = [held([P, S], U32, f"v_w{a}") for a in range(2)]
        nc.vector.tensor_copy(v_s[:], tab_s[:].indirect(idx[:]))
        for q in range(4):
            nc.sync.dma_start(v_s_last[32 * q : 32 * q + 4].bitcast(I32), v_s[32 * q + 4 : 32 * q + 8].bitcast(I32))

        nc.sync.dma_start(idx2[:], offs2)
        nc.sync.dma_start(gain[:], wgs)
        nc.sync.dma_start(wo_w[:], wo_words[0].rearrange("p c i -> p (c i)").bitcast(I32))
        load_scale_rows(nc.sync, wo_s, wo_scales)
        nc.sync.dma_start(idx3[:], offs3)
        for c in range(M // CHUNK):
            cols = slice(CHUNK * c, CHUNK * (c + 1))
            nc.sync.dma_start(cap[c][:], ceiling[:, cols].rearrange("(p t) m -> p t m", t=PACK))
            for g in range(2):
                rows = shift[PASS * g : PASS * (g + 1), cols]
                nc.sync.dma_start(y[c][g][:], rows.rearrange("(p t) m -> p t m", t=PACK))

        wp_c = held([P, 2, H], U32, "wp_c")
        wp_s = held([P, 2, H], U8, "wp_s")

        def quantise_wp(n, copy):
            a, c0, w = wp_parts[n]
            grouped = held([P, w, PACK], BF16, f"wp_bf{n}")
            copy(interleaved(grouped[:]), by_rows(wp_raw[n][:]))
            nc.vector.quantize_mx(
                out=wp_c[:, a, c0 : c0 + w].bitcast(FP8X4),
                scales=wp_s[:, a, c0 : c0 + w],
                in_=grouped[:].rearrange("p c t -> p (c t)"),
            )

        nc.vector.tensor_copy(v_w[0][:], tab_w[0][:].indirect(idx[:]))
        quantise_wp(0, nc.scalar.copy)
        quantise_wp(1, nc.scalar.copy)
        start = 0
        for count in LAST_PASS_GATHERS:
            nc.vector.tensor_copy(v_w[1][:, start : start + count], tab_w[1][:].indirect(entries(idx, start, count)))
            start = start + count

        def add_turned(out, first, second):
            nc.tensor.matmul(out, first, ident[:], start=True, stop=False, is_transpose=True)
            nc.tensor.matmul(out, second, ident[:], start=False, stop=True, is_transpose=True)

        def terms(block, parts):
            cols = slice(P * block, P * (block + 1))
            ang = psum.tile([P, H], F32, name="ang", tag="acc", bufs=6)
            amp = psum.tile([P, H], F32, name="amp", tag="acc", bufs=6)
            first, last = (0, 1) if block == 0 else (1, 0)
            for a in (first, last):
                nc.tensor.matmul_mx(
                    out=ang[:], lhsT=v_w[a][:, cols].bitcast(FP8X4), lhsT_scale=(v_s, v_s_last)[a][:, cols],
                    rhs=wq_w[:, a, :].bitcast(FP4X4), rhs_scale=wq_s[:, a, :], start=(a == first), stop=(a == last),
                )
            for a in (first, last):
                nc.tensor.matmul_mx(
                    out=amp[:], lhsT=v_w[a][:, cols].bitcast(FP8X4), lhsT_scale=v_s[4 * a : P, cols],
                    rhs=wp_c[:, a, :].bitcast(FP8X4), rhs_scale=wp_s[:, a, :], start=(a == first), stop=(a == last),
                )
            pos = ring.tile([P, PACK, P], F32, name="pos", bufs=4)
            neg = ring.tile([P, PACK, P], F32, name="neg", bufs=4)
            ang_dealt = ang[:].rearrange("j (q i) -> j i q", i=PACK)
            amp_dealt = amp[:].rearrange("j (q i) -> j i q", i=PACK)
            for n, rows in enumerate(parts):
                if block == 0:
                    sq = keep.tile([P, rows.stop - rows.start, P], F32, name="sq", tag=f"dealt{n}", align_bytes=64)
                else:
                    sq = ring.tile([P, PACK, P], F32, name="sq")
                nc.scalar.activation(sq[:], ang_dealt[:, rows, :], ACT.Sin, scale=0.5)
                nc.scalar.activation(sq[:], sq[:], ACT.Square)
                nc.scalar.activation(pos[:, rows, :], amp_dealt[:, rows, :], ACT.Relu, scale=2.0)
                nc.vector.scalar_tensor_tensor(neg[:, rows, :], amp_dealt[:, rows, :], -2.0, sq[:], ALU.mult, ALU.mult)
            return pos, neg

        def turn_back(pos, neg, h_cols, parts):
            for rows in parts:
                turned = psum.tile([P, PACK, P], F32, name="turned", bufs=2)
                for i in range(rows.start, rows.stop):
                    add_turned(turned[:, i, :], pos[:, i, :], neg[:, i, :])
                nc.scalar.copy(h_cols[:, rows, :], turned[:, rows, :])

        whole = [slice(0, PACK)]
        halves = [slice(0, PACK // 2), slice(PACK // 2, PACK)]
        starts = [sum(SCATTER_WIDTHS[:n]) for n in range(len(SCATTER_WIDTHS) + 1)]
        made = {}

        def make_terms(upto):
            for block in range(len(made), min(upto, S) // P):
                made[block] = terms(block, halves if block == 0 else whole)

        for n, count in enumerate(SCATTER_WIDTHS):
            start = starts[n]
            make_terms(start + count + (0 if n == 0 else 2 * P))
            h = ring.tile([P, PACK, count], F32, name="h", bufs=3)
            for b in range(count // P):
                block = start // P + b
                turn_back(*made[block], h[:, :, P * b : P * (b + 1)], halves if block == 0 else whole)
            for i in range(PACK):
                nc.vector.tensor_tensor(
                    pages[i][:].indirect(entries(idx2, start, count)), h[:, i, :], gain[:, start : start + count],
                    ALU.mult,
                )

        wo_ds = keep.tile([P, N], U8, name="wo_ds", tag="dealt0", align_bytes=64)
        wo_dw = keep.tile([P, N], I32, name="wo_dw", tag="dealt1", align_bytes=64)
        nc.vector.tensor_copy(
            wo_dw[:].rearrange("p (g t b q) -> p g b t q", g=2, t=PACK, q=PACK),
            wo_w[:].rearrange("p (g b q t) -> p g b t q", g=2, t=PACK, q=PACK),
        )
        nc.vector.tensor_copy(
            wo_ds[:].rearrange("p (g t q) -> p g t q", g=2, t=PACK),
            wo_s[:, 0, :].rearrange("p (g q t) -> p g t q", g=2, t=PACK),
        )

        shift_turned = {}
        for c in range(TURNED_CHUNKS):
            for b in range(CHUNK // P):
                turned = psum.tile([P, PACK, P], F32, name="turned", bufs=2)
                for t in range(PACK):
                    nc.tensor.transpose(turned[:, t, :], y[c][0][:, t, P * b : P * (b + 1)], ident[:])
                shift_turned[c, b] = held([P, PACK, P], F32, f"shift_turned{c}_{b}")
                nc.scalar.copy(shift_turned[c, b][:], turned[:])

        y_s = held([P, 2, M], U8, "y_s")

        def add_on_vector(z_c, z_s, g, y_part):
            width = y_part.shape[2]
            per_bank = H // width
            for t0 in range(0, PACK, per_bank):
                acc = psum.tile([P, per_bank, width], F32, name="acc", tag="acc", bufs=6)
                for u in range(per_bank):
                    n0 = PASS * g + P * (t0 + u)
                    nc.tensor.matmul_mx(
                        out=acc[:, u, :], lhsT=wo_dw[:, n0 : n0 + P].bitcast(FP8X4), lhsT_scale=wo_ds[:, n0 : n0 + P],
                        rhs=z_c.bitcast(FP8X4), rhs_scale=z_s, start=True, stop=True,
                    )
                rows = y_part[:, t0 : t0 + per_bank, :]
                nc.vector.tensor_tensor(rows, acc[:], rows, ALU.add)

        def add_on_tensor(z_c, z_s, c):
            products = []
            for b in range(CHUNK // P):
                cols = slice(P * b, P * (b + 1))
                acc = psum.tile([P, PASS], F32, name="acc", tag="acc", bufs=6)
                nc.tensor.matmul_mx(
                    out=acc[:], lhsT=z_c[:, cols].bitcast(FP8X4), lhsT_scale=z_s[:, cols],
                    rhs=wo_w[:, 0:PASS].bitcast(FP8X4), rhs_scale=wo_s[:, 0, 0:PASS], start=True, stop=True,
                )
                product = ring.tile([P, PACK, P], F32, name="product")
                nc.scalar.copy(product[:], acc[:].rearrange("m (q t) -> m t q", t=PACK))
                products.append(product)
            for t0 in range(0, PACK, 2):
                turned = psum.tile([P, 2, CHUNK], F32, name="turned", bufs=2)
                for u in range(2):
                    for b in range(CHUNK // P):
                        add_turned(
                            turned[:, u, P * b : P * (b + 1)], products[b][:, t0 + u, :], shift_turned[c, b][:, t0 + u, :]
                        )
                nc.scalar.copy(y[c][0][:, t0 : t0 + 2, :], turned[:])

        def hand_out(y_part, g, cols, copy, tag, bufs):
            width = y_part.shape[2]
            nc.sync.dma_start(out_0[PASS * g : PASS * (g + 1), cols].rearrange("(p t) m -> p t m", t=PACK), y_part)
            y_grouped = ring.tile([P, width, PACK], BF16, name="y_grouped", align_bytes=64, tag=tag, bufs=bufs)
            copy(interleaved(y_grouped[:]), by_rows(y_part))
            y_c = ring.tile([P, width], U32, name="y_c", align_bytes=64, bufs=4)
            nc.vector.quantize_mx(
                out=y_c[:].bitcast(FP8X4), scales=y_s[:, g, cols], in_=y_grouped[:].rearrange("p c t -> p (c t)")
            )
            nc.sync.dma_start(out_1[g, :, cols, :].rearrange("p m t -> p (m t)").bitcast(I32), y_c[:].bitcast(I32))

        step = 0
        for c in range(M // CHUNK):
            x = ring.tile([P, PACK, CHUNK], F32, name="x", bufs=1)
            for i in range(PACK):
                nc.vector.tensor_copy(x[:, i, :], pages[i][:].indirect(entries(idx3, CHUNK * c, CHUNK)))
            width = CHUNK if c < TURNED_CHUNKS else CHUNK // 2
            for m0 in range(0, CHUNK, width):
                part = slice(m0, m0 + width)
                cols = slice(CHUNK * c + m0, CHUNK * c + m0 + width)
                last = CHUNK * c + m0 + width == M
                shared = "grouped_last" if last else f"grouped{step % 2}"
                step = step + 1
                z_grouped = ring.tile([P, width, PACK], BF16, name="z_grouped", align_bytes=64, tag=shared, bufs=1)
                nc.vector.tensor_tensor(
                    interleaved(z_grouped[:], 2), by_rows(x[:, :, part], 2), by_rows(cap[c][:, :, part], 2), ALU.min
                )
                z_c = ring.tile([P, width], U32, name="z_c", align_bytes=64)
                z_s = ring.tile([P, width], U8, name="z_s", align_bytes=64)
                nc.vector.quantize_mx(
                    out=z_c[:].bitcast(FP8X4), scales=z_s[:], in_=z_grouped[:].rearrange("p c t -> p (c t)")
                )
                for g in range(2):
                    if g == 0 and c < TURNED_CHUNKS:
                        add_on_tensor(z_c, z_s, c)
                    else:
                        add_on_vector(z_c[:], z_s[:], g, y[c][g][:, :, part])
                    copy = nc.vector.tensor_copy if last and g == 1 else nc.scalar.copy
                    hand_out(y[c][g][:, :, part], g, cols, copy, *((shared, 1) if g == 0 else ("grouped_second", 2)))
        for q in range(4):
            nc.scalar.dma_start(
                out_2[:, 4 * q : 4 * q + 4, :].rearrange("g r m -> r g m").bitcast(I32),
                y_s[32 * q : 32 * q + 4].bitcast(I32),
            )
